import numpy as np
CORES = [23,119,17,113]
N = 4
F = 64
TK = N * F
EPS = 0.01
def setup_inputs(rng):
    return {"x": rng.standard_normal((N, 128, TK), dtype=np.float32) * (0.5 + np.abs(rng.standard_normal((1, 1, TK), dtype=np.float32)))}
def setup_inputs_big(rng):
    d = setup_inputs(rng)
    for k in ("x",): d[k] = (d[k].astype(np.float32) * 1024.0).astype(d[k].dtype)
    return d
def setup_inputs_small(rng):
    d = setup_inputs(rng)
    for k in ("x",): d[k] = (d[k].astype(np.float32) * (1 / 1024.0)).astype(d[k].dtype)
    return d
def setup_inputs_apart(rng):
    d = setup_inputs(rng)
    f = (10.0 ** rng.permutation(np.linspace(-1.5, 1.5, N))).astype(np.float32).reshape(N, 1, 1)
    for k in ("x",): d[k] = (d[k].astype(np.float32) * f).astype(d[k].dtype)
    return d
def setup_inputs_mixed(rng):
    d = setup_inputs(rng)
    f = (10.0 ** rng.uniform(-3, 3, (1, 1, TK))).astype(np.float32); shape = rng.integers(2, size=(1, 1, TK))
    for k in ("x",):
        x = d[k].astype(np.float32)
        other = x * np.where(rng.random((1, 128, TK)) < 0.5, 0.1, 1.0).astype(np.float32)
        d[k] = (np.where(shape == 1, other, x) * f).astype(d[k].dtype)
    return d
def reference(x):
    s = x.astype(np.float64).sum(axis=0)
    n = s / np.sqrt((s ** 2).sum(axis=0) / 128 + EPS)
    return {"y": np.broadcast_to(n.astype(np.float32), (N, 128, TK))}

@@ -1,0 +1,163 @@
+import math
+from concourse.bass import DstId, RemoteDMATransfer
+from concourse.mybir import AluOpType, ActivationFunctionType
+
+D = 128
+TK = 256
+EPS = 0.01
+WIDTHS = [128, 128]
+NB = len(WIDTHS)
+STARTS = [sum(WIDTHS[:j]) for j in range(NB)]
+C = 2.0 ** -23
+KAPPA = C * math.sqrt(float(D))
+
+SCRATCH = {
+    "X": ("sbuf", [D, TK], "float32"),
+    "L0": ("sbuf", [D, TK], "float32"),
+    "L1": ("sbuf", [D, TK], "float32"),
+    "L2": ("sbuf", [D, TK], "float32"),
+    "S": ("sbuf", [D, TK], "float32"),
+    "SQ": ("sbuf", [D, TK], "float32"),
+    "Y": ("sbuf", [D, TK], "float32"),
+    "DG": ("sbuf", [D, TK], "float32"),
+    "ONES": ("sbuf", [D, D], "float32"),
+    "IDN": ("sbuf", [D, D], "float32"),
+    "EPSW": ("sbuf", [D, 4], "float32"),
+    "Q": ("sbuf", [D, 4 * NB], "float32"),
+    "R0": ("sbuf", [D, 4 * NB], "float32"),
+    "TT": ("sbuf", [D, 4 * NB], "float32"),
+    "U": ("sbuf", [D, 4 * NB], "float32"),
+    "P": ("psum", [D, 512], "float32"),
+}
+for _j in range(NB):
+    SCRATCH["V%d" % _j] = ("psum", [D, 512], "float32")
+    SCRATCH["RB%d" % _j] = ("psum", [D, 512], "float32")
+
+SEMAPHORES = ["k", "idn", "sent", "st"]
+for _j in range(NB):
+    SEMAPHORES += ["ld%d" % _j, "c%d" % _j, "a0_%d" % _j, "a1_%d" % _j, "a2_%d" % _j]
+
+PRE, ADD1, ADD2, SQD, SSD, RTD, RCD, N1D, N2D, DGD, RBD, MUL = range(1, 13)
+
+
+def _bits(mask):
+    return [b for b in range(mask.bit_length()) if (mask >> b) & 1]
+
+
+def _mask(bits):
+    m = 0
+    for b in bits:
+        m |= 1 << b
+    return m
+
+
+def _order(topo, cores, dst):
+    peers = [q for q in cores if q != dst]
+    return ([q for q in peers if topo.chip(q) == topo.chip(dst)]
+            + [q for q in peers if topo.chip(q) != topo.chip(dst)])
+
+
+def rank_program(g, core, T, topo):
+    if T.rank_of(core) is None:
+        return
+    sem = T.sem
+    add, mult = AluOpType.add, AluOpType.mult
+    Act = ActivationFunctionType
+    V, S, PE, SY = g.vector, g.scalar, g.tensor, g.sync
+    cols = [slice(STARTS[j], STARTS[j] + WIDTHS[j]) for j in range(NB)]
+    cj = [sem["c%d" % j] for j in range(NB)]
+    ld = [sem["ld%d" % j] for j in range(NB)]
+
+    peers = _order(topo, T.cores, core)
+    near = [q for q in peers if topo.chip(q) == topo.chip(core)]
+    far = [q for q in peers if topo.chip(q) != topo.chip(core)]
+    assert len(near) == 1 and len(far) == 2 and all(topo.may_write(core, q) for q in peers)
+    far_bits = _bits(topo.mask(core, far[0]) & topo.mask(core, far[1]))
+    half = len(far_bits) // 2
+    eng = {far[0]: far_bits[:half], far[1]: far_bits[half:]}
+    eng[near[0]] = [b for b in _bits(topo.mask(core, near[0])) if b not in far_bits]
+    n_near, n_far = len(eng[near[0]]), half
+
+    def transfer(q, j):
+        slot = _order(topo, T.cores, q).index(core)
+        rid, pid, _ = topo.addr(q)
+        return RemoteDMATransfer(dst_ids=[DstId(rid=rid, pnc=pid)], dma_engine_mask=_mask(eng[q]),
+                                 remote_sem=sem["a%d_%d" % (slot, j)],
+                                 src=T.X[:, cols[j]], dst=T["L%d" % slot][:, cols[j]])
+
+    for j in range(NB):
+        (SY if j % 2 == 0 else S).dma_start(T.X[:, cols[j]], T.x[:, cols[j]]).then_inc(ld[j], 16)
+
+    sent = 0
+    for j in range(NB):
+        g.wait_ge(ld[j], 16)
+        g.remote_dma_fused([transfer(q, j) for q in far], local_sem=sem.sent)
+        g.remote_dma_fused([transfer(q, j) for q in near], local_sem=sem.sent)
+        sent += 2 * n_far + n_near
+    g.wait_ge(sem.k, 2)
+    g.affine_select(T.IDN[:], T.ONES[:], [[-1, D]], AluOpType.is_equal, 0.0, 0, 1).then_inc(sem.idn, 1)
+    g.wait_ge(sem.sent, sent)
+
+    V.memset(T.ONES[:], 1.0).then_inc(sem.k, 1)
+    V.memset(T.EPSW[:], float(D) * C * C * EPS).then_inc(sem.k, 1)
+    for j in range(NB):
+        V.wait_ge(ld[j], 16)
+        V.wait_ge(sem["a0_%d" % j], n_near)
+        V.tensor_tensor(T.P[:, cols[j]], T.X[:, cols[j]], T.L0[:, cols[j]], add).then_inc(cj[j], 1)
+
+    def v_adds(j):
+        V.wait_ge(cj[j], PRE)
+        V.wait_ge(sem["a1_%d" % j], n_far)
+        V.tensor_tensor(T.P[:, cols[j]], T.P[:, cols[j]], T.L1[:, cols[j]], add).then_inc(cj[j], 1)
+        V.wait_ge(cj[j], ADD1)
+        V.wait_ge(sem["a2_%d" % j], n_far)
+        V.tensor_tensor(T.S[:, cols[j]], T.P[:, cols[j]], T.L2[:, cols[j]], add).then_inc(cj[j], 1)
+
+    def v_small(j):
+        w = WIDTHS[j]
+        k = slice(4 * j, 4 * j + 1)
+        V.wait_ge(cj[j], RTD)
+        V.reciprocal(T.R0[0:w, k], T.Q[0:w, k]).then_inc(cj[j], 1)
+        V.wait_ge(cj[j], RCD)
+        V.tensor_scalar(T.TT[0:w, k], T.R0[0:w, k], T.R0[0:w, k], T["V%d" % j][0:w, 0:1], mult, mult).then_inc(cj[j], 1)
+        V.wait_ge(cj[j], N1D)
+        V.tensor_scalar(T.U[0:w, k], T.TT[0:w, k], -0.5 * KAPPA, 1.5 * KAPPA, mult, add).then_inc(cj[j], 1)
+        V.wait_ge(cj[j], N2D)
+        V.wait_ge(sem.idn, 1)
+        V.tensor_scalar(T.DG[0:w, cols[j]], T.IDN[0:w, 0:w], T.R0[0:w, k], T.U[0:w, k], mult, mult).then_inc(cj[j], 1)
+
+    def v_mul(j):
+        V.wait_ge(cj[j], RBD)
+        V.tensor_tensor(T.Y[:, cols[j]], T.S[:, cols[j]], T["RB%d" % j][:, 0:WIDTHS[j]], mult).then_inc(cj[j], 1)
+
+    for j in range(NB):
+        v_adds(j)
+    for j in range(NB):
+        v_small(j)
+    for j in range(NB):
+        v_mul(j)
+
+    for j in range(NB):
+        w = WIDTHS[j]
+        S.wait_ge(cj[j], ADD2)
+        S.activation(T.SQ[:, cols[j]], T.S[:, cols[j]], Act.Square, scale=C).then_inc(cj[j], 1)
+        S.wait_ge(cj[j], SSD)
+        S.activation(T.Q[0:w, 4 * j:4 * j + 1], T["V%d" % j][0:w, 0:1], Act.Sqrt).then_inc(cj[j], 1)
+
+    PE.wait_ge(sem.k, 2)
+    for j in range(NB):
+        w = WIDTHS[j]
+        PE.matmul(T["V%d" % j][0:w, 0:1], T.ONES[0:1, 0:w], T.EPSW[0:1, 0:1], True, False)
+    for j in range(NB):
+        w = WIDTHS[j]
+        PE.wait_ge(cj[j], SQD)
+        PE.matmul(T["V%d" % j][0:w, 0:1], T.SQ[:, cols[j]], T.ONES[:, 0:1], False, True).then_inc(cj[j], 1)
+    for j in range(NB):
+        w = WIDTHS[j]
+        PE.wait_ge(cj[j], DGD)
+        PE.matmul(T["RB%d" % j][:, 0:w], T.ONES[0:w, :], T.DG[0:w, cols[j]], True, True).then_inc(cj[j], 1)
+
+    for j in range(NB):
+        SY.wait_ge(cj[j], MUL)
+        SY.dma_start(T.y[:, cols[j]], T.Y[:, cols[j]]).then_inc(sem.st, 16)
+    SY.wait_ge(sem.st, 16 * NB)

@@ -15,29 +15,35 @@ SCRATCH = {
     "X": ("sbuf", [D, TK], "float32"),
     "L0": ("sbuf", [D, TK], "float32"),
     "L1": ("sbuf", [D, TK], "float32"),
-    "L2": ("sbuf", [D, TK], "float32"),
+    "L2": ("sbuf", [D, WIDTHS[0]], "float32"),
+    "CS": ("sbuf", [D, WIDTHS[1]], "float32"),
     "S": ("sbuf", [D, TK], "float32"),
     "SQ": ("sbuf", [D, TK], "float32"),
     "Y": ("sbuf", [D, TK], "float32"),
     "DG": ("sbuf", [D, TK], "float32"),
     "ONES": ("sbuf", [D, D], "float32"),
-    "IDN": ("sbuf", [D, D], "float32"),
+    "KF": ("sbuf", [D, D], "float32"),
+    "IDK": ("sbuf", [D, D], "float32"),
     "EPSW": ("sbuf", [D, 4], "float32"),
-    "Q": ("sbuf", [D, 4 * NB], "float32"),
-    "R0": ("sbuf", [D, 4 * NB], "float32"),
-    "TT": ("sbuf", [D, 4 * NB], "float32"),
-    "U": ("sbuf", [D, 4 * NB], "float32"),
+    "CC": ("sbuf", [D, 4], "float32"),
+    "DA": ("sbuf", [D, 4 * NB], "float32"),
+    "DB": ("sbuf", [D, 4], "float32"),
+    "DO": ("sbuf", [D, 4 * NB], "float32"),
     "P": ("psum", [D, 512], "float32"),
 }
 for _j in range(NB):
-    SCRATCH["V%d" % _j] = ("psum", [D, 512], "float32")
+    SCRATCH["VA%d" % _j] = ("psum", [D, 512], "float32")
+    SCRATCH["VB%d" % _j] = ("psum", [D, 512], "float32")
     SCRATCH["RB%d" % _j] = ("psum", [D, 512], "float32")
 
-SEMAPHORES = ["k", "idn", "sent", "st"]
+SEMAPHORES = ["k", "idn", "sent", "st", "a2_0"]
 for _j in range(NB):
-    SEMAPHORES += ["ld%d" % _j, "c%d" % _j, "a0_%d" % _j, "a1_%d" % _j, "a2_%d" % _j]
+    SEMAPHORES += ["ld%d" % _j, "c%d" % _j, "vb%d" % _j, "q%d" % _j, "a0_%d" % _j, "a1_%d" % _j]
 
-PRE, ADD1, ADD2, SQD, SSD, RTD, RCD, N1D, N2D, DGD, RBD, MUL = range(1, 13)
+PRE, ADD1, ADD2, SQD, SSA = range(1, 6)
+SSB, RWD = 1, 2
+RTD, SCD, DGD, RBD, MUL = range(1, 6)
+NK = 6
 
 
 def _bits(mask):
@@ -66,98 +72,114 @@ def rank_program(g, core, T, topo):
     V, S, PE, SY = g.vector, g.scalar, g.tensor, g.sync
     cols = [slice(STARTS[j], STARTS[j] + WIDTHS[j]) for j in range(NB)]
     cj = [sem["c%d" % j] for j in range(NB)]
+    vb = [sem["vb%d" % j] for j in range(NB)]
+    qj = [sem["q%d" % j] for j in range(NB)]
     ld = [sem["ld%d" % j] for j in range(NB)]
 
     peers = _order(topo, T.cores, core)
     near = [q for q in peers if topo.chip(q) == topo.chip(core)]
     far = [q for q in peers if topo.chip(q) != topo.chip(core)]
     assert len(near) == 1 and len(far) == 2 and all(topo.may_write(core, q) for q in peers)
+    twin = [q for q in far if topo.die(q) == topo.die(core)]
+    assert len(twin) == 1
     far_bits = _bits(topo.mask(core, far[0]) & topo.mask(core, far[1]))
     half = len(far_bits) // 2
     eng = {far[0]: far_bits[:half], far[1]: far_bits[half:]}
     eng[near[0]] = [b for b in _bits(topo.mask(core, near[0])) if b not in far_bits]
-    n_near, n_far = len(eng[near[0]]), half
+    n_near, n_far, n_all = len(eng[near[0]]), half, len(far_bits)
 
     def transfer(q, j):
         slot = _order(topo, T.cores, q).index(core)
         rid, pid, _ = topo.addr(q)
+        dst = T.L2[:] if slot == 2 else T["L%d" % slot][:, cols[j]]
         return RemoteDMATransfer(dst_ids=[DstId(rid=rid, pnc=pid)], dma_engine_mask=_mask(eng[q]),
-                                 remote_sem=sem["a%d_%d" % (slot, j)],
-                                 src=T.X[:, cols[j]], dst=T["L%d" % slot][:, cols[j]])
+                                 remote_sem=sem["a%d_%d" % (slot, j)], src=T.X[:, cols[j]], dst=dst)
 
-    for j in range(NB):
-        (SY if j % 2 == 0 else S).dma_start(T.X[:, cols[j]], T.x[:, cols[j]]).then_inc(ld[j], 16)
+    SY.dma_start(T.X[:, cols[0]], T.x[:, cols[0]]).then_inc(ld[0], 16)
+    S.dma_start(T.X[:, cols[1]], T.x[:, cols[1]]).then_inc(ld[1], 16)
 
-    sent = 0
-    for j in range(NB):
-        g.wait_ge(ld[j], 16)
-        g.remote_dma_fused([transfer(q, j) for q in far], local_sem=sem.sent)
-        g.remote_dma_fused([transfer(q, j) for q in near], local_sem=sem.sent)
-        sent += 2 * n_far + n_near
-    g.wait_ge(sem.k, 2)
-    g.affine_select(T.IDN[:], T.ONES[:], [[-1, D]], AluOpType.is_equal, 0.0, 0, 1).then_inc(sem.idn, 1)
-    g.wait_ge(sem.sent, sent)
+    g.wait_ge(ld[0], 16)
+    g.remote_dma_fused([transfer(q, 0) for q in far], local_sem=sem.sent)
+    g.wait_ge(ld[1], 16)
+    g.remote_dma_fused([transfer(near[0], 1)], local_sem=sem.sent)
+    g.remote_dma_fused([transfer(near[0], 0)], local_sem=sem.sent)
+    g.wait_ge(cj[1], PRE)
+    rid, pid, _ = topo.addr(twin[0])
+    g.remote_dma_fused([RemoteDMATransfer(dst_ids=[DstId(rid=rid, pnc=pid)], dma_engine_mask=_mask(far_bits),
+                                          remote_sem=sem.a1_1, src=T.CS[:], dst=T.L1[:, cols[1]])],
+                       local_sem=sem.sent)
+    g.wait_ge(sem.k, NK)
+    g.affine_select(T.IDK[:], T.KF[:], [[-1, D]], AluOpType.is_equal, 0.0, 0, 1).then_inc(sem.idn, 1)
+    g.wait_ge(sem.sent, 2 * n_far + 2 * n_near + n_all)
 
     V.memset(T.ONES[:], 1.0).then_inc(sem.k, 1)
     V.memset(T.EPSW[:], float(D) * C * C * EPS).then_inc(sem.k, 1)
-    for j in range(NB):
-        V.wait_ge(ld[j], 16)
-        V.wait_ge(sem["a0_%d" % j], n_near)
-        V.tensor_tensor(T.P[:, cols[j]], T.X[:, cols[j]], T.L0[:, cols[j]], add).then_inc(cj[j], 1)
-
-    def v_adds(j):
-        V.wait_ge(cj[j], PRE)
-        V.wait_ge(sem["a1_%d" % j], n_far)
-        V.tensor_tensor(T.P[:, cols[j]], T.P[:, cols[j]], T.L1[:, cols[j]], add).then_inc(cj[j], 1)
-        V.wait_ge(cj[j], ADD1)
-        V.wait_ge(sem["a2_%d" % j], n_far)
-        V.tensor_tensor(T.S[:, cols[j]], T.P[:, cols[j]], T.L2[:, cols[j]], add).then_inc(cj[j], 1)
-
-    def v_small(j):
-        w = WIDTHS[j]
-        k = slice(4 * j, 4 * j + 1)
-        V.wait_ge(cj[j], RTD)
-        V.reciprocal(T.R0[0:w, k], T.Q[0:w, k]).then_inc(cj[j], 1)
-        V.wait_ge(cj[j], RCD)
-        V.tensor_scalar(T.TT[0:w, k], T.R0[0:w, k], T.R0[0:w, k], T["V%d" % j][0:w, 0:1], mult, mult).then_inc(cj[j], 1)
-        V.wait_ge(cj[j], N1D)
-        V.tensor_scalar(T.U[0:w, k], T.TT[0:w, k], -0.5 * KAPPA, 1.5 * KAPPA, mult, add).then_inc(cj[j], 1)
-        V.wait_ge(cj[j], N2D)
-        V.wait_ge(sem.idn, 1)
-        V.tensor_scalar(T.DG[0:w, cols[j]], T.IDN[0:w, 0:w], T.R0[0:w, k], T.U[0:w, k], mult, mult).then_inc(cj[j], 1)
-
-    def v_mul(j):
-        V.wait_ge(cj[j], RBD)
-        V.tensor_tensor(T.Y[:, cols[j]], T.S[:, cols[j]], T["RB%d" % j][:, 0:WIDTHS[j]], mult).then_inc(cj[j], 1)
-
-    for j in range(NB):
-        v_adds(j)
-    for j in range(NB):
-        v_small(j)
-    for j in range(NB):
-        v_mul(j)
-
+    V.memset(T.CC[:], C * C).then_inc(sem.k, 1)
+    V.memset(T.KF[:], -0.5 * KAPPA).then_inc(sem.k, 1)
+    V.memset(T.DB[:, 0:1], 0.0).then_inc(sem.k, 1)
+    V.memset(T.DB[:, 1:2], -3.0).then_inc(sem.k, 1)
+    V.wait_ge(sem.k, NK)
+    V.wait_ge(ld[1], 16)
+    V.wait_ge(sem.a0_1, n_near)
+    V.tensor_tensor(T.CS[:], T.X[:, cols[1]], T.L0[:, cols[1]], add).then_inc(cj[1], 1)
+    V.wait_ge(ld[0], 16)
+    V.wait_ge(sem.a0_0, n_near)
+    V.tensor_tensor(T.P[:, cols[0]], T.X[:, cols[0]], T.L0[:, cols[0]], add).then_inc(cj[0], 1)
+    V.wait_ge(cj[1], PRE)
+    V.tensor_copy(T.P[:, cols[1]], T.CS[:]).then_inc(cj[1], 1)
+    V.wait_ge(cj[0], PRE)
+    V.wait_ge(sem.a1_0, n_far)
+    V.tensor_tensor(T.P[:, cols[0]], T.P[:, cols[0]], T.L1[:, cols[0]], add).then_inc(cj[0], 1)
+    V.wait_ge(cj[0], ADD1)
+    V.wait_ge(sem.a2_0, n_far)
+    V.tensor_tensor(T.S[:, cols[0]], T.P[:, cols[0]], T.L2[:], add).then_inc(cj[0], 1)
+    V.wait_ge(cj[1], ADD1)
+    V.wait_ge(sem.a1_1, n_all)
+    V.tensor_tensor(T.S[:, cols[1]], T.P[:, cols[1]], T.L1[:, cols[1]], add).then_inc(cj[1], 1)
+    V.wait_ge(cj[1], ADD2)
+    V.tensor_tensor(T.SQ[:, cols[1]], T.S[:, cols[1]], T.S[:, cols[1]], mult).then_inc(cj[1], 1)
     for j in range(NB):
         w = WIDTHS[j]
-        S.wait_ge(cj[j], ADD2)
-        S.activation(T.SQ[:, cols[j]], T.S[:, cols[j]], Act.Square, scale=C).then_inc(cj[j], 1)
-        S.wait_ge(cj[j], SSD)
-        S.activation(T.Q[0:w, 4 * j:4 * j + 1], T["V%d" % j][0:w, 0:1], Act.Sqrt).then_inc(cj[j], 1)
+        V.wait_ge(vb[j], SSB)
+        V.reciprocal(T.DA[0:w, 4 * j:4 * j + 1], T["VB%d" % j][0:w, 0:1]).then_inc(vb[j], 1)
+    V.wait_ge(sem.idn, 1)
+    for j in range(NB):
+        w = WIDTHS[j]
+        V.wait_ge(vb[j], RWD)
+        V.wait_ge(qj[j], RTD)
+        V.tensor_tensor_scan(T.DO[0:w, 4 * j:4 * j + 2], T.DA[0:w, 4 * j:4 * j + 2], T.DB[0:w, 0:2],
+                             T.DA[0:w, 4 * j + 1:4 * j + 2], mult, add).then_inc(qj[j], 1)
+        V.wait_ge(qj[j], SCD)
+        V.tensor_scalar(T.DG[0:w, cols[j]], T.IDK[0:w, 0:w], T.DO[0:w, 4 * j:4 * j + 1],
+                        T.DO[0:w, 4 * j + 1:4 * j + 2], mult, mult).then_inc(qj[j], 1)
+    for j in range(NB):
+        V.wait_ge(qj[j], RBD)
+        V.tensor_tensor(T.Y[:, cols[j]], T.S[:, cols[j]], T["RB%d" % j][:, 0:WIDTHS[j]], mult).then_inc(qj[j], 1)
 
-    PE.wait_ge(sem.k, 2)
+    S.wait_ge(cj[0], ADD2)
+    S.activation(T.SQ[:, cols[0]], T.S[:, cols[0]], Act.Square, scale=C).then_inc(cj[0], 1)
     for j in range(NB):
         w = WIDTHS[j]
-        PE.matmul(T["V%d" % j][0:w, 0:1], T.ONES[0:1, 0:w], T.EPSW[0:1, 0:1], True, False)
+        S.wait_ge(cj[j], SSA)
+        S.activation(T.DA[0:w, 4 * j + 1:4 * j + 2], T["VA%d" % j][0:w, 0:1], Act.Sqrt).then_inc(qj[j], 1)
+
+    PE.wait_ge(sem.k, NK)
     for j in range(NB):
         w = WIDTHS[j]
+        PE.matmul(T["VA%d" % j][0:w, 0:1], T.ONES[0:1, 0:w], T.EPSW[0:1, 0:1], True, False)
+        PE.matmul(T["VB%d" % j][0:w, 0:1], T.ONES[0:1, 0:w], T.EPSW[0:1, 0:1], True, False)
+    for j in range(NB):
+        w = WIDTHS[j]
+        col = T.ONES[:, 0:1] if j == 0 else T.CC[:, 0:1]
         PE.wait_ge(cj[j], SQD)
-        PE.matmul(T["V%d" % j][0:w, 0:1], T.SQ[:, cols[j]], T.ONES[:, 0:1], False, True).then_inc(cj[j], 1)
+        PE.matmul(T["VA%d" % j][0:w, 0:1], T.SQ[:, cols[j]], col, False, True).then_inc(cj[j], 1)
+        PE.matmul(T["VB%d" % j][0:w, 0:1], T.SQ[:, cols[j]], col, False, True).then_inc(vb[j], 1)
     for j in range(NB):
         w = WIDTHS[j]
-        PE.wait_ge(cj[j], DGD)
-        PE.matmul(T["RB%d" % j][:, 0:w], T.ONES[0:w, :], T.DG[0:w, cols[j]], True, True).then_inc(cj[j], 1)
+        PE.wait_ge(qj[j], DGD)
+        PE.matmul(T["RB%d" % j][:, 0:w], T.ONES[0:w, :], T.DG[0:w, cols[j]], True, True).then_inc(qj[j], 1)
 
     for j in range(NB):
-        SY.wait_ge(cj[j], MUL)
+        SY.wait_ge(qj[j], MUL)
         SY.dma_start(T.y[:, cols[j]], T.Y[:, cols[j]]).then_inc(sem.st, 16)
     SY.wait_ge(sem.st, 16 * NB)

@@ -10,6 +10,7 @@ NB = len(WIDTHS)
 STARTS = [sum(WIDTHS[:j]) for j in range(NB)]
 C = 2.0 ** -23
 KAPPA = C * math.sqrt(float(D))
+LS = 4 + D
 
 SCRATCH = {
     "X": ("sbuf", [D, TK], "float32"),
@@ -20,18 +21,17 @@ SCRATCH = {
     "S": ("sbuf", [D, TK], "float32"),
     "SQ": ("sbuf", [D, TK], "float32"),
     "Y": ("sbuf", [D, TK], "float32"),
-    "DG": ("sbuf", [D, TK], "float32"),
     "ONES": ("sbuf", [D, D], "float32"),
     "KF": ("sbuf", [D, D], "float32"),
     "IDK": ("sbuf", [D, D], "float32"),
     "EPSW": ("sbuf", [D, 4], "float32"),
     "CC": ("sbuf", [D, 4], "float32"),
-    "DA": ("sbuf", [D, 4 * NB], "float32"),
-    "DB": ("sbuf", [D, 4], "float32"),
-    "DO": ("sbuf", [D, 4 * NB], "float32"),
+    "DB": ("sbuf", [D, LS], "float32"),
     "P": ("psum", [D, 512], "float32"),
 }
 for _j in range(NB):
+    SCRATCH["DA%d" % _j] = ("sbuf", [D, LS], "float32")
+    SCRATCH["DO%d" % _j] = ("sbuf", [D, LS], "float32")
     SCRATCH["VA%d" % _j] = ("psum", [D, 512], "float32")
     SCRATCH["VB%d" % _j] = ("psum", [D, 512], "float32")
     SCRATCH["RB%d" % _j] = ("psum", [D, 512], "float32")
@@ -41,9 +41,9 @@ for _j in range(NB):
     SEMAPHORES += ["ld%d" % _j, "c%d" % _j, "vb%d" % _j, "q%d" % _j, "a0_%d" % _j, "a1_%d" % _j]
 
 PRE, ADD1, ADD2, SQD, SSA = range(1, 6)
-SSB, RWD = 1, 2
-RTD, SCD, DGD, RBD, MUL = range(1, 6)
-NK = 6
+SSB, RWD = 1, 3
+RTD, SCD, RBD, MUL = range(1, 5)
+NK = 9
 
 
 def _bits(mask):
@@ -55,12 +55,6 @@ def _mask(bits):
     for b in bits:
         m |= 1 << b
     return m
-
-
-def _order(topo, cores, dst):
-    peers = [q for q in cores if q != dst]
-    return ([q for q in peers if topo.chip(q) == topo.chip(dst)]
-            + [q for q in peers if topo.chip(q) != topo.chip(dst)])
 
 
 def rank_program(g, core, T, topo):
@@ -75,42 +69,42 @@ def rank_program(g, core, T, topo):
     vb = [sem["vb%d" % j] for j in range(NB)]
     qj = [sem["q%d" % j] for j in range(NB)]
     ld = [sem["ld%d" % j] for j in range(NB)]
+    DA = [T["DA%d" % j] for j in range(NB)]
+    DO = [T["DO%d" % j] for j in range(NB)]
+    VA = [T["VA%d" % j] for j in range(NB)]
+    VB = [T["VB%d" % j] for j in range(NB)]
+    RB = [T["RB%d" % j] for j in range(NB)]
 
-    peers = _order(topo, T.cores, core)
+    peers = [q for q in T.cores if q != core]
     near = [q for q in peers if topo.chip(q) == topo.chip(core)]
     far = [q for q in peers if topo.chip(q) != topo.chip(core)]
     assert len(near) == 1 and len(far) == 2 and all(topo.may_write(core, q) for q in peers)
     twin = [q for q in far if topo.die(q) == topo.die(core)]
-    assert len(twin) == 1
+    cross = [q for q in far if topo.die(q) != topo.die(core)]
+    assert len(twin) == 1 and len(cross) == 1
     far_bits = _bits(topo.mask(core, far[0]) & topo.mask(core, far[1]))
-    half = len(far_bits) // 2
-    eng = {far[0]: far_bits[:half], far[1]: far_bits[half:]}
-    eng[near[0]] = [b for b in _bits(topo.mask(core, near[0])) if b not in far_bits]
-    n_near, n_far, n_all = len(eng[near[0]]), half, len(far_bits)
+    near_bits = [b for b in _bits(topo.mask(core, near[0])) if b not in far_bits]
+    n_near, n_all = len(near_bits), len(far_bits)
 
-    def transfer(q, j):
-        slot = _order(topo, T.cores, q).index(core)
+    def write(q, bits, rsem, src, dst):
         rid, pid, _ = topo.addr(q)
-        dst = T.L2[:] if slot == 2 else T["L%d" % slot][:, cols[j]]
-        return RemoteDMATransfer(dst_ids=[DstId(rid=rid, pnc=pid)], dma_engine_mask=_mask(eng[q]),
-                                 remote_sem=sem["a%d_%d" % (slot, j)], src=T.X[:, cols[j]], dst=dst)
+        g.remote_dma_fused([RemoteDMATransfer(dst_ids=[DstId(rid=rid, pnc=pid)], dma_engine_mask=_mask(bits),
+                                              remote_sem=rsem, src=src, dst=dst)], local_sem=sem.sent)
 
     SY.dma_start(T.X[:, cols[0]], T.x[:, cols[0]]).then_inc(ld[0], 16)
     S.dma_start(T.X[:, cols[1]], T.x[:, cols[1]]).then_inc(ld[1], 16)
 
     g.wait_ge(ld[0], 16)
-    g.remote_dma_fused([transfer(q, 0) for q in far], local_sem=sem.sent)
+    write(twin[0], far_bits, sem.a1_0, T.X[:, cols[0]], T.L1[:, cols[0]])
+    write(cross[0], far_bits, sem.a2_0, T.X[:, cols[0]], T.L2[:])
     g.wait_ge(ld[1], 16)
-    g.remote_dma_fused([transfer(near[0], 1)], local_sem=sem.sent)
-    g.remote_dma_fused([transfer(near[0], 0)], local_sem=sem.sent)
+    write(near[0], near_bits, sem.a0_1, T.X[:, cols[1]], T.L0[:, cols[1]])
+    write(near[0], near_bits, sem.a0_0, T.X[:, cols[0]], T.L0[:, cols[0]])
     g.wait_ge(cj[1], PRE)
-    rid, pid, _ = topo.addr(twin[0])
-    g.remote_dma_fused([RemoteDMATransfer(dst_ids=[DstId(rid=rid, pnc=pid)], dma_engine_mask=_mask(far_bits),
-                                          remote_sem=sem.a1_1, src=T.CS[:], dst=T.L1[:, cols[1]])],
-                       local_sem=sem.sent)
+    write(twin[0], far_bits, sem.a1_1, T.CS[:], T.L1[:, cols[1]])
     g.wait_ge(sem.k, NK)
     g.affine_select(T.IDK[:], T.KF[:], [[-1, D]], AluOpType.is_equal, 0.0, 0, 1).then_inc(sem.idn, 1)
-    g.wait_ge(sem.sent, 2 * n_far + 2 * n_near + n_all)
+    g.wait_ge(sem.sent, 3 * n_all + 2 * n_near)
 
     V.memset(T.ONES[:], 1.0).then_inc(sem.k, 1)
     V.memset(T.EPSW[:], float(D) * C * C * EPS).then_inc(sem.k, 1)
@@ -118,6 +112,9 @@ def rank_program(g, core, T, topo):
     V.memset(T.KF[:], -0.5 * KAPPA).then_inc(sem.k, 1)
     V.memset(T.DB[:, 0:1], 0.0).then_inc(sem.k, 1)
     V.memset(T.DB[:, 1:2], -3.0).then_inc(sem.k, 1)
+    V.memset(T.DB[:, 2:LS], 0.0).then_inc(sem.k, 1)
+    for j in range(NB):
+        V.memset(DA[j][:, 4:LS], 1.0).then_inc(sem.k, 1)
     V.wait_ge(sem.k, NK)
     V.wait_ge(ld[1], 16)
     V.wait_ge(sem.a0_1, n_near)
@@ -128,10 +125,10 @@ def rank_program(g, core, T, topo):
     V.wait_ge(cj[1], PRE)
     V.tensor_copy(T.P[:, cols[1]], T.CS[:]).then_inc(cj[1], 1)
     V.wait_ge(cj[0], PRE)
-    V.wait_ge(sem.a1_0, n_far)
+    V.wait_ge(sem.a1_0, n_all)
     V.tensor_tensor(T.P[:, cols[0]], T.P[:, cols[0]], T.L1[:, cols[0]], add).then_inc(cj[0], 1)
     V.wait_ge(cj[0], ADD1)
-    V.wait_ge(sem.a2_0, n_far)
+    V.wait_ge(sem.a2_0, n_all)
     V.tensor_tensor(T.S[:, cols[0]], T.P[:, cols[0]], T.L2[:], add).then_inc(cj[0], 1)
     V.wait_ge(cj[1], ADD1)
     V.wait_ge(sem.a1_1, n_all)
@@ -139,45 +136,36 @@ def rank_program(g, core, T, topo):
     V.wait_ge(cj[1], ADD2)
     V.tensor_tensor(T.SQ[:, cols[1]], T.S[:, cols[1]], T.S[:, cols[1]], mult).then_inc(cj[1], 1)
     for j in range(NB):
-        w = WIDTHS[j]
         V.wait_ge(vb[j], SSB)
-        V.reciprocal(T.DA[0:w, 4 * j:4 * j + 1], T["VB%d" % j][0:w, 0:1]).then_inc(vb[j], 1)
-    V.wait_ge(sem.idn, 1)
+        V.reciprocal(DA[j][:, 0:1], VB[j][:, 0:1]).then_inc(vb[j], 1)
+        V.reciprocal(DA[j][:, 3:4], VB[j][:, 0:1]).then_inc(vb[j], 1)
     for j in range(NB):
-        w = WIDTHS[j]
         V.wait_ge(vb[j], RWD)
         V.wait_ge(qj[j], RTD)
-        V.tensor_tensor_scan(T.DO[0:w, 4 * j:4 * j + 2], T.DA[0:w, 4 * j:4 * j + 2], T.DB[0:w, 0:2],
-                             T.DA[0:w, 4 * j + 1:4 * j + 2], mult, add).then_inc(qj[j], 1)
-        V.wait_ge(qj[j], SCD)
-        V.tensor_scalar(T.DG[0:w, cols[j]], T.IDK[0:w, 0:w], T.DO[0:w, 4 * j:4 * j + 1],
-                        T.DO[0:w, 4 * j + 1:4 * j + 2], mult, mult).then_inc(qj[j], 1)
+        V.tensor_tensor_scan(DO[j][:, 0:LS], DA[j][:, 0:LS], T.DB[:, 0:LS], DA[j][:, 1:2], mult, add).then_inc(qj[j], 1)
     for j in range(NB):
         V.wait_ge(qj[j], RBD)
-        V.tensor_tensor(T.Y[:, cols[j]], T.S[:, cols[j]], T["RB%d" % j][:, 0:WIDTHS[j]], mult).then_inc(qj[j], 1)
+        V.tensor_tensor(T.Y[:, cols[j]], T.S[:, cols[j]], RB[j][:, 0:D], mult).then_inc(qj[j], 1)
 
     S.wait_ge(cj[0], ADD2)
     S.activation(T.SQ[:, cols[0]], T.S[:, cols[0]], Act.Square, scale=C).then_inc(cj[0], 1)
     for j in range(NB):
-        w = WIDTHS[j]
         S.wait_ge(cj[j], SSA)
-        S.activation(T.DA[0:w, 4 * j + 1:4 * j + 2], T["VA%d" % j][0:w, 0:1], Act.Sqrt).then_inc(qj[j], 1)
+        S.activation(DA[j][:, 1:3], VA[j][:, 0:2], Act.Sqrt).then_inc(qj[j], 1)
 
     PE.wait_ge(sem.k, NK)
     for j in range(NB):
-        w = WIDTHS[j]
-        PE.matmul(T["VA%d" % j][0:w, 0:1], T.ONES[0:1, 0:w], T.EPSW[0:1, 0:1], True, False)
-        PE.matmul(T["VB%d" % j][0:w, 0:1], T.ONES[0:1, 0:w], T.EPSW[0:1, 0:1], True, False)
+        PE.matmul(VA[j][:, 0:2], T.ONES[0:1, :], T.EPSW[0:1, 0:2], True, False)
+        PE.matmul(VB[j][:, 0:1], T.ONES[0:1, :], T.EPSW[0:1, 0:1], True, False)
     for j in range(NB):
-        w = WIDTHS[j]
-        col = T.ONES[:, 0:1] if j == 0 else T.CC[:, 0:1]
+        col = T.ONES if j == 0 else T.CC
         PE.wait_ge(cj[j], SQD)
-        PE.matmul(T["VA%d" % j][0:w, 0:1], T.SQ[:, cols[j]], col, False, True).then_inc(cj[j], 1)
-        PE.matmul(T["VB%d" % j][0:w, 0:1], T.SQ[:, cols[j]], col, False, True).then_inc(vb[j], 1)
+        PE.matmul(VA[j][:, 0:2], T.SQ[:, cols[j]], col[:, 0:2], False, True).then_inc(cj[j], 1)
+        PE.matmul(VB[j][:, 0:1], T.SQ[:, cols[j]], col[:, 0:1], False, True).then_inc(vb[j], 1)
+    PE.wait_ge(sem.idn, 1)
     for j in range(NB):
-        w = WIDTHS[j]
-        PE.wait_ge(qj[j], DGD)
-        PE.matmul(T["RB%d" % j][:, 0:w], T.ONES[0:w, :], T.DG[0:w, cols[j]], True, True).then_inc(qj[j], 1)
+        PE.wait_ge(qj[j], SCD)
+        PE.matmul(RB[j][:, 0:D], DO[j][:, 4:LS], T.IDK[:], True, True).then_inc(qj[j], 1)
 
     for j in range(NB):
         SY.wait_ge(qj[j], MUL)

import math
from concourse.bass import DstId, RemoteDMATransfer
from concourse.mybir import AluOpType, ActivationFunctionType

D = 128
TK = 256
EPS = 0.01
WIDTHS = [128, 128]
NB = len(WIDTHS)
STARTS = [sum(WIDTHS[:j]) for j in range(NB)]
C = 2.0 ** -23
KAPPA = C * math.sqrt(float(D))
LS = 4 + D

SCRATCH = {
    "X": ("sbuf", [D, TK], "float32"),
    "L0": ("sbuf", [D, TK], "float32"),
    "L1": ("sbuf", [D, TK], "float32"),
    "L2": ("sbuf", [D, WIDTHS[0]], "float32"),
    "CS": ("sbuf", [D, WIDTHS[1]], "float32"),
    "S": ("sbuf", [D, TK], "float32"),
    "SQ": ("sbuf", [D, TK], "float32"),
    "Y": ("sbuf", [D, TK], "float32"),
    "ONES": ("sbuf", [D, D], "float32"),
    "KF": ("sbuf", [D, D], "float32"),
    "IDK": ("sbuf", [D, D], "float32"),
    "EPSW": ("sbuf", [D, 4], "float32"),
    "CC": ("sbuf", [D, 4], "float32"),
    "DB": ("sbuf", [D, LS], "float32"),
    "P": ("psum", [D, 512], "float32"),
}
for _j in range(NB):
    SCRATCH["DA%d" % _j] = ("sbuf", [D, LS], "float32")
    SCRATCH["DO%d" % _j] = ("sbuf", [D, LS], "float32")
    SCRATCH["VA%d" % _j] = ("psum", [D, 512], "float32")
    SCRATCH["VB%d" % _j] = ("psum", [D, 512], "float32")
    SCRATCH["RB%d" % _j] = ("psum", [D, 512], "float32")

SEMAPHORES = ["k", "idn", "sent", "st", "a2_0"]
for _j in range(NB):
    SEMAPHORES += ["ld%d" % _j, "c%d" % _j, "vb%d" % _j, "q%d" % _j, "a0_%d" % _j, "a1_%d" % _j]

PRE, ADD1, ADD2, SQD, SSA = range(1, 6)
SSB, RWD = 1, 3
RTD, SCD, RBD, MUL = range(1, 5)
NK = 9


def _bits(mask):
    return [b for b in range(mask.bit_length()) if (mask >> b) & 1]


def _mask(bits):
    m = 0
    for b in bits:
        m |= 1 << b
    return m


def rank_program(g, core, T, topo):
    if T.rank_of(core) is None:
        return
    sem = T.sem
    add, mult = AluOpType.add, AluOpType.mult
    Act = ActivationFunctionType
    V, S, PE, SY = g.vector, g.scalar, g.tensor, g.sync
    cols = [slice(STARTS[j], STARTS[j] + WIDTHS[j]) for j in range(NB)]
    cj = [sem["c%d" % j] for j in range(NB)]
    vb = [sem["vb%d" % j] for j in range(NB)]
    qj = [sem["q%d" % j] for j in range(NB)]
    ld = [sem["ld%d" % j] for j in range(NB)]
    DA = [T["DA%d" % j] for j in range(NB)]
    DO = [T["DO%d" % j] for j in range(NB)]
    VA = [T["VA%d" % j] for j in range(NB)]
    VB = [T["VB%d" % j] for j in range(NB)]
    RB = [T["RB%d" % j] for j in range(NB)]

    peers = [q for q in T.cores if q != core]
    near = [q for q in peers if topo.chip(q) == topo.chip(core)]
    far = [q for q in peers if topo.chip(q) != topo.chip(core)]
    assert len(near) == 1 and len(far) == 2 and all(topo.may_write(core, q) for q in peers)
    twin = [q for q in far if topo.die(q) == topo.die(core)]
    cross = [q for q in far if topo.die(q) != topo.die(core)]
    assert len(twin) == 1 and len(cross) == 1
    far_bits = _bits(topo.mask(core, far[0]) & topo.mask(core, far[1]))
    near_bits = [b for b in _bits(topo.mask(core, near[0])) if b not in far_bits]
    n_near, n_all = len(near_bits), len(far_bits)

    def write(q, bits, rsem, src, dst):
        rid, pid, _ = topo.addr(q)
        g.remote_dma_fused([RemoteDMATransfer(dst_ids=[DstId(rid=rid, pnc=pid)], dma_engine_mask=_mask(bits),
                                              remote_sem=rsem, src=src, dst=dst)], local_sem=sem.sent)

    SY.dma_start(T.X[:, cols[0]], T.x[:, cols[0]]).then_inc(ld[0], 16)
    S.dma_start(T.X[:, cols[1]], T.x[:, cols[1]]).then_inc(ld[1], 16)

    g.wait_ge(ld[0], 16)
    write(twin[0], far_bits, sem.a1_0, T.X[:, cols[0]], T.L1[:, cols[0]])
    write(cross[0], far_bits, sem.a2_0, T.X[:, cols[0]], T.L2[:])
    g.wait_ge(ld[1], 16)
    write(near[0], near_bits, sem.a0_1, T.X[:, cols[1]], T.L0[:, cols[1]])
    write(near[0], near_bits, sem.a0_0, T.X[:, cols[0]], T.L0[:, cols[0]])
    g.wait_ge(cj[1], PRE)
    write(twin[0], far_bits, sem.a1_1, T.CS[:], T.L1[:, cols[1]])
    g.wait_ge(sem.k, NK)
    g.affine_select(T.IDK[:], T.KF[:], [[-1, D]], AluOpType.is_equal, 0.0, 0, 1).then_inc(sem.idn, 1)
    g.wait_ge(sem.sent, 3 * n_all + 2 * n_near)

    V.memset(T.ONES[:], 1.0).then_inc(sem.k, 1)
    V.memset(T.EPSW[:], float(D) * C * C * EPS).then_inc(sem.k, 1)
    V.memset(T.CC[:], C * C).then_inc(sem.k, 1)
    V.memset(T.KF[:], -0.5 * KAPPA).then_inc(sem.k, 1)
    V.memset(T.DB[:, 0:1], 0.0).then_inc(sem.k, 1)
    V.memset(T.DB[:, 1:2], -3.0).then_inc(sem.k, 1)
    V.memset(T.DB[:, 2:LS], 0.0).then_inc(sem.k, 1)
    for j in range(NB):
        V.memset(DA[j][:, 4:LS], 1.0).then_inc(sem.k, 1)
    V.wait_ge(sem.k, NK)
    V.wait_ge(ld[1], 16)
    V.wait_ge(sem.a0_1, n_near)
    V.tensor_tensor(T.CS[:], T.X[:, cols[1]], T.L0[:, cols[1]], add).then_inc(cj[1], 1)
    V.wait_ge(ld[0], 16)
    V.wait_ge(sem.a0_0, n_near)
    V.tensor_tensor(T.P[:, cols[0]], T.X[:, cols[0]], T.L0[:, cols[0]], add).then_inc(cj[0], 1)
    V.wait_ge(cj[1], PRE)
    V.tensor_copy(T.P[:, cols[1]], T.CS[:]).then_inc(cj[1], 1)
    V.wait_ge(cj[0], PRE)
    V.wait_ge(sem.a1_0, n_all)
    V.tensor_tensor(T.P[:, cols[0]], T.P[:, cols[0]], T.L1[:, cols[0]], add).then_inc(cj[0], 1)
    V.wait_ge(cj[0], ADD1)
    V.wait_ge(sem.a2_0, n_all)
    V.tensor_tensor(T.S[:, cols[0]], T.P[:, cols[0]], T.L2[:], add).then_inc(cj[0], 1)
    V.wait_ge(cj[1], ADD1)
    V.wait_ge(sem.a1_1, n_all)
    V.tensor_tensor(T.S[:, cols[1]], T.P[:, cols[1]], T.L1[:, cols[1]], add).then_inc(cj[1], 1)
    V.wait_ge(cj[1], ADD2)
    V.tensor_tensor(T.SQ[:, cols[1]], T.S[:, cols[1]], T.S[:, cols[1]], mult).then_inc(cj[1], 1)
    for j in range(NB):
        V.wait_ge(vb[j], SSB)
        V.reciprocal(DA[j][:, 0:1], VB[j][:, 0:1]).then_inc(vb[j], 1)
        V.reciprocal(DA[j][:, 3:4], VB[j][:, 0:1]).then_inc(vb[j], 1)
    for j in range(NB):
        V.wait_ge(vb[j], RWD)
        V.wait_ge(qj[j], RTD)
        V.tensor_tensor_scan(DO[j][:, 0:LS], DA[j][:, 0:LS], T.DB[:, 0:LS], DA[j][:, 1:2], mult, add).then_inc(qj[j], 1)
    for j in range(NB):
        V.wait_ge(qj[j], RBD)
        V.tensor_tensor(T.Y[:, cols[j]], T.S[:, cols[j]], RB[j][:, 0:D], mult).then_inc(qj[j], 1)

    S.wait_ge(cj[0], ADD2)
    S.activation(T.SQ[:, cols[0]], T.S[:, cols[0]], Act.Square, scale=C).then_inc(cj[0], 1)
    for j in range(NB):
        S.wait_ge(cj[j], SSA)
        S.activation(DA[j][:, 1:3], VA[j][:, 0:2], Act.Sqrt).then_inc(qj[j], 1)

    PE.wait_ge(sem.k, NK)
    for j in range(NB):
        PE.matmul(VA[j][:, 0:2], T.ONES[0:1, :], T.EPSW[0:1, 0:2], True, False)
        PE.matmul(VB[j][:, 0:1], T.ONES[0:1, :], T.EPSW[0:1, 0:1], True, False)
    for j in range(NB):
        col = T.ONES if j == 0 else T.CC
        PE.wait_ge(cj[j], SQD)
        PE.matmul(VA[j][:, 0:2], T.SQ[:, cols[j]], col[:, 0:2], False, True).then_inc(cj[j], 1)
        PE.matmul(VB[j][:, 0:1], T.SQ[:, cols[j]], col[:, 0:1], False, True).then_inc(vb[j], 1)
    PE.wait_ge(sem.idn, 1)
    for j in range(NB):
        PE.wait_ge(qj[j], SCD)
        PE.matmul(RB[j][:, 0:D], DO[j][:, 4:LS], T.IDK[:], True, True).then_inc(qj[j], 1)

    for j in range(NB):
        SY.wait_ge(qj[j], MUL)
        SY.dma_start(T.y[:, cols[j]], T.Y[:, cols[j]]).then_inc(sem.st, 16)
    SY.wait_ge(sem.st, 16 * NB)
